import numpy as np
import ml_dtypes


def mxq(x, axis, fmt="e4m3"):
    dtype, down = {"e4m3": (ml_dtypes.float8_e4m3fn, 7), "e5m2": (ml_dtypes.float8_e5m2, 14)}[fmt]
    v = np.moveaxis(np.asarray(x, np.float32).astype(ml_dtypes.bfloat16).astype(np.float64), axis, -1)
    blocks = v.reshape(v.shape[:-1] + (-1, 32))
    amax = np.abs(blocks).max(-1, keepdims=True)
    byte = np.maximum(np.where(amax > 0, np.frexp(amax)[1] - 1 + 127, 0) - down, 1)
    scale = np.exp2(byte - 127.0)
    codes = (blocks / scale).astype(np.float32).astype(dtype).astype(np.float64)
    return np.moveaxis((codes * scale).reshape(v.shape), -1, axis)


WIDE = False


def mx_kscale(k):
    if not WIDE:
        return np.ones(k)
    levels = np.array([30, -30])
    if k % 512:
        return np.exp2(np.random.permutation(np.resize(levels, k // 32))).repeat(32)
    a = np.empty((k // 512, 16))
    for p in range(k // 512):
        a[p, :8] = np.random.permutation(np.resize(levels, 8))
        for g in range(8):
            far = levels[np.abs(levels - a[p, g]) >= 10]
            a[p, g + 8] = far[np.random.randint(len(far))]
    return np.exp2(a.ravel()).repeat(32)


def f64(x):
    return np.asarray(x).astype(np.float64)


def striped(idx):
    return np.tile(idx.reshape(-1, 16).T, (8, 1)).astype(np.uint16)


def unstriped(offs):
    return offs[:16].T.reshape(-1).astype(np.int64)


def d_relu2(v):
    return 2.0 * np.maximum(v, 0.0)


K, T, E, C, H, N = 256, 1024, 2, 512, 512, 512


def by_expert(wq, xq):
    return np.concatenate([wq[e].T @ xq[:, e * C:(e + 1) * C] for e in range(E)], axis=1)


def setup_inputs():
    n = np.random.standard_normal
    s = mx_kscale(N)[:, None]
    u = mx_kscale(H)
    return {
        "dyT": (n((N, T)) * s).astype(np.float32),
        "a": n((H, E * C)).astype(np.float32),
        "w2": (n((E, N, H)) / np.sqrt(N) / s[None] * u[None, None, :]).astype(np.float32),
        "w1": (n((E, H, K)) / np.sqrt(H) / u[None, :, None]).astype(np.float32),
        "gate": np.tile(np.random.uniform(0.2, 1.0, E * C), (N, 1)).astype(np.float32),
        "offs": striped(np.random.permutation(T)[:E * C]),
    }


def reference(dyT, a, w2, w1, gate, offs):
    idx = unstriped(offs)
    gq = mxq(f64(gate) * f64(dyT)[:, idx], 0, "e5m2")
    dh = by_expert(mxq(f64(w2), 1, "e4m3"), gq)
    da = dh * d_relu2(f64(a))
    dx = by_expert(mxq(f64(w1), 1, "e4m3"), mxq(da, 0, "e5m2"))
    out = np.zeros((K, T))
    out[:, idx] = dx
    return out

@@ -1,0 +1,195 @@
+from contextlib import ExitStack
+
+import concourse.mybir as mybir
+
+K, T, E, C, H, N = 256, 1024, 2, 512, 512, 512
+FLOPS = 2 * E * C * (N * H + H * K)
+BYTES = 4 * (N * T + H * E * C + E * N * H + E * H * K + E * C + K * T) + 2 * T * 8
+
+F32 = mybir.dt.float32
+BF16 = mybir.dt.bfloat16
+U32 = mybir.dt.uint32
+U16 = mybir.dt.uint16
+U8 = mybir.dt.uint8
+E4M3X4 = mybir.dt.float8_e4m3fn_x4
+E5M2X4 = mybir.dt.float8_e5m2_x4
+MULT = mybir.AluOpType.mult
+MAX = mybir.AluOpType.max
+COPY = mybir.ActivationFunctionType.Copy
+
+P = 128
+J = 4
+
+
+def tile_moe_bdx_mlp_relu2_kernel(tc, dyT, a, w2, w1, gate, offs, out):
+    nc = tc.nc
+    with ExitStack() as ctx:
+        keep = ctx.enter_context(tc.tile_pool(name="keep", bufs=1))
+        psum = ctx.enter_context(tc.psum_pool(name="psum", bufs=1))
+
+        def sb(shape, dtype, name):
+            return keep.tile(shape, dtype, name=name, align_bytes=64)
+
+        offsets = keep.tile([P, T // 16], U16, name="offsets")
+        gates = [sb([P, C], F32, f"gate{e}") for e in range(E)]
+        dy = [sb([P, T], F32, f"dy{j}") for j in range(J)]
+        w2_raw = [sb([P, J, H], F32, f"w2_raw{e}") for e in range(E)]
+        w1_raw = [sb([P, J, K], F32, f"w1_raw{e}") for e in range(E)]
+        a_raw = [sb([P, J, C], F32, f"a_raw{e}") for e in range(E)]
+
+        dyv = dyT.rearrange("(p j) t -> j p t", j=J)
+        av = a.rearrange("(p j) s -> p j s", j=J)
+
+        def slots(e):
+            return slice(e * C, (e + 1) * C)
+
+        def load_gate(e):
+            nc.sync.dma_start(out=gates[e][:], in_=gate[0:P, slots(e)])
+
+        def load_w2(e):
+            nc.sync.dma_start(out=w2_raw[e][:], in_=w2[e].rearrange("(p j) i -> p j i", j=J))
+
+        def load_w1(e):
+            nc.sync.dma_start(out=w1_raw[e][:], in_=w1[e].rearrange("(p j) k -> p j k", j=J))
+
+        def load_a(e):
+            nc.sync.dma_start(out=a_raw[e][:], in_=av[:, :, slots(e)])
+
+        nc.sync.dma_start(offsets[:], offs)
+        load_gate(0)
+        for j in range(J):
+            nc.sync.dma_start(out=dy[j][:], in_=dyv[j])
+        load_gate(1)
+        load_w2(0)
+        load_a(0)
+        load_w2(1)
+        load_w1(0)
+        load_a(1)
+        load_w1(1)
+
+        g4 = [sb([P, J, C], F32, f"g4_{e}") for e in range(E)]
+        gb = [sb([P, C, J], BF16, f"gb{e}") for e in range(E)]
+        gq = [sb([P, C], U32, f"gq{e}") for e in range(E)]
+        gs = [sb([P, C], U8, f"gs{e}") for e in range(E)]
+        w2b = [sb([P, J, P, J], BF16, f"w2b{e}") for e in range(E)]
+        w2q = [sb([P, H], U32, f"w2q{e}") for e in range(E)]
+        w2s = [sb([P, H], U8, f"w2s{e}") for e in range(E)]
+        w1b = [sb([P, K, J], BF16, f"w1b{e}") for e in range(E)]
+        w1q = [sb([P, K], U32, f"w1q{e}") for e in range(E)]
+        w1s = [sb([P, K], U8, f"w1s{e}") for e in range(E)]
+        da4 = [sb([P, J, C], BF16, f"da4_{e}") for e in range(E)]
+        dab = [sb([P, C, J], BF16, f"dab{e}") for e in range(E)]
+        daq = [sb([P, C], U32, f"daq{e}") for e in range(E)]
+        das = [sb([P, C], U8, f"das{e}") for e in range(E)]
+        dx = [[sb([P, C], F32, f"dx{e}_{m}") for m in range(2)] for e in range(E)]
+        outs = [sb([P, T], F32, f"outs{m}") for m in range(2)]
+
+        def offs_of(e):
+            return offsets[:, e * (C // 16) : (e + 1) * (C // 16)]
+
+        def gather(e, j):
+            nc.vector.tensor_tensor(g4[e][:, j, :], dy[j][:].indirect(offs_of(e)), gates[e][:], MULT)
+
+        def interleave(copy, dst, src):
+            copy(out=dst.rearrange("p (c i) t -> p c t i", i=4), in_=src.rearrange("p t (c i) -> p c t i", i=4))
+
+        def group_w2(copy, e, t0, t1):
+            copy(out=w2b[e][:, t0:t1], in_=w2_raw[e][:].rearrange("p j (m t) -> p t m j", t=4)[:, t0:t1])
+
+        def quantize(codes, scales, src, fmt):
+            nc.vector.quantize_mx(out=codes[:].bitcast(fmt), scales=scales[:], in_=src)
+
+        def quant_w2(e):
+            quantize(w2q[e], w2s[e], w2b[e][:].rearrange("p t m j -> p (t m j)"), E4M3X4)
+
+        def quant_w1(e):
+            quantize(w1q[e], w1s[e], w1b[e][:].rearrange("p k j -> p (k j)"), E4M3X4)
+
+        def quant_g(e):
+            quantize(gq[e], gs[e], gb[e][:].rearrange("p c j -> p (c j)"), E5M2X4)
+
+        def quant_da(e):
+            quantize(daq[e], das[e], dab[e][:].rearrange("p c j -> p (c j)"), E5M2X4)
+
+        def first_product(e):
+            banks = []
+            for t in range(J):
+                bank = psum.tile([P, C], F32, name=f"dh{e}_{t}", tag=f"bank{4 * e + t}")
+                cols = slice(t * P, (t + 1) * P)
+                nc.tensor.matmul_mx(
+                    out=bank[:],
+                    lhsT=w2q[e][:, cols].bitcast(E4M3X4),
+                    lhsT_scale=w2s[e][:, cols],
+                    rhs=gq[e][:].bitcast(E5M2X4),
+                    rhs_scale=gs[e][:],
+                    start=True,
+                    stop=True,
+                )
+                banks.append(bank)
+            return banks
+
+        def make_da(e, banks):
+            for t in range(J):
+                nc.vector.scalar_tensor_tensor(
+                    out=da4[e][:, t, :], in0=a_raw[e][:, t, :], scalar=0.0, in1=banks[t][:], op0=MAX, op1=MULT
+                )
+
+        def second_product(e):
+            for m in range(2):
+                bank = psum.tile([P, C], F32, name=f"dxp{e}_{m}", tag=f"bank{4 * e + m}")
+                cols = slice(m * P, (m + 1) * P)
+                nc.tensor.matmul_mx(
+                    out=bank[:],
+                    lhsT=w1q[e][:, cols].bitcast(E4M3X4),
+                    lhsT_scale=w1s[e][:, cols],
+                    rhs=daq[e][:].bitcast(E5M2X4),
+                    rhs_scale=das[e][:],
+                    start=True,
+                    stop=True,
+                )
+                nc.scalar.activation(dx[e][m][:], bank[:], COPY, scale=2.0)
+
+        def scatter(e, m):
+            nc.vector.tensor_copy(outs[m][:].indirect(offs_of(e)), dx[e][m][:])
+
+        scopy = nc.scalar.copy
+        vcopy = nc.vector.tensor_copy
+
+        half = C // 2
+
+        def interleave_shared(dst, src):
+            interleave(vcopy, dst[:, :half, :], src[:, :, :half])
+            interleave(scopy, dst[:, half:, :], src[:, :, half:])
+
+        for j in range(J):
+            gather(0, j)
+        interleave(scopy, gb[0][:], g4[0][:])
+        group_w2(vcopy, 0, 0, 2)
+        group_w2(scopy, 0, 2, 4)
+        quant_w2(0)
+        quant_g(0)
+        dh = first_product(0)
+        make_da(0, dh)
+        interleave_shared(dab[0][:], da4[0][:])
+        quant_da(0)
+        interleave(scopy, w1b[0][:], w1_raw[0][:])
+        quant_w1(0)
+        second_product(0)
+        for j in range(J):
+            gather(1, j)
+        interleave(scopy, gb[1][:], g4[1][:])
+        group_w2(scopy, 1, 0, 4)
+        quant_w2(1)
+        quant_g(1)
+        dh = first_product(1)
+        make_da(1, dh)
+        interleave_shared(dab[1][:], da4[1][:])
+        interleave(scopy, w1b[1][:], w1_raw[1][:])
+        quant_w1(1)
+        scatter(0, 0)
+        quant_da(1)
+        scatter(0, 1)
+        second_product(1)
+        for m in range(2):
+            scatter(1, m)
+            nc.sync.dma_start(out=out[m * P : (m + 1) * P, :], in_=outs[m][:])

@@ -19,6 +19,7 @@ COPY = mybir.ActivationFunctionType.Copy
 
 P = 128
 J = 4
+DX_BANK = ((0, 7), (1, 2))
 
 
 def tile_moe_bdx_mlp_relu2_kernel(tc, dyT, a, w2, w1, gate, offs, out):
@@ -61,11 +62,11 @@ def tile_moe_bdx_mlp_relu2_kernel(tc, dyT, a, w2, w1, gate, offs, out):
             nc.sync.dma_start(out=dy[j][:], in_=dyv[j])
         load_gate(1)
         load_w2(0)
+        load_w1(0)
+        load_w1(1)
         load_a(0)
         load_w2(1)
-        load_w1(0)
         load_a(1)
-        load_w1(1)
 
         g4 = [sb([P, J, C], F32, f"g4_{e}") for e in range(E)]
         gb = [sb([P, C, J], BF16, f"gb{e}") for e in range(E)]
@@ -93,8 +94,11 @@ def tile_moe_bdx_mlp_relu2_kernel(tc, dyT, a, w2, w1, gate, offs, out):
         def interleave(copy, dst, src):
             copy(out=dst.rearrange("p (c i) t -> p c t i", i=4), in_=src.rearrange("p t (c i) -> p c t i", i=4))
 
-        def group_w2(copy, e, t0, t1):
-            copy(out=w2b[e][:, t0:t1], in_=w2_raw[e][:].rearrange("p j (m t) -> p t m j", t=4)[:, t0:t1])
+        def group_w2(copy, e, m0, m1):
+            copy(
+                out=w2b[e][:].rearrange("p t m j -> p m j t")[:, m0:m1],
+                in_=w2_raw[e][:].rearrange("p j (m t) -> p m j t", t=4)[:, m0:m1],
+            )
 
         def quantize(codes, scales, src, fmt):
             nc.vector.quantize_mx(out=codes[:].bitcast(fmt), scales=scales[:], in_=src)
@@ -128,15 +132,16 @@ def tile_moe_bdx_mlp_relu2_kernel(tc, dyT, a, w2, w1, gate, offs, out):
                 banks.append(bank)
             return banks
 
-        def make_da(e, banks):
-            for t in range(J):
+        def make_da(e, banks, ts=range(J)):
+            for t in ts:
                 nc.vector.scalar_tensor_tensor(
                     out=da4[e][:, t, :], in0=a_raw[e][:, t, :], scalar=0.0, in1=banks[t][:], op0=MAX, op1=MULT
                 )
 
         def second_product(e):
+            sums = []
             for m in range(2):
-                bank = psum.tile([P, C], F32, name=f"dxp{e}_{m}", tag=f"bank{4 * e + m}")
+                bank = psum.tile([P, C], F32, name=f"dxp{e}_{m}", tag=f"bank{DX_BANK[e][m]}")
                 cols = slice(m * P, (m + 1) * P)
                 nc.tensor.matmul_mx(
                     out=bank[:],
@@ -147,7 +152,11 @@ def tile_moe_bdx_mlp_relu2_kernel(tc, dyT, a, w2, w1, gate, offs, out):
                     start=True,
                     stop=True,
                 )
-                nc.scalar.activation(dx[e][m][:], bank[:], COPY, scale=2.0)
+                sums.append(bank)
+            return sums
+
+        def emit_dx(e, m, sums):
+            nc.scalar.activation(dx[e][m][:], sums[m][:], COPY, scale=2.0)
 
         def scatter(e, m):
             nc.vector.tensor_copy(outs[m][:].indirect(offs_of(e)), dx[e][m][:])
@@ -161,35 +170,49 @@ def tile_moe_bdx_mlp_relu2_kernel(tc, dyT, a, w2, w1, gate, offs, out):
             interleave(vcopy, dst[:, :half, :], src[:, :, :half])
             interleave(scopy, dst[:, half:, :], src[:, :, half:])
 
+        half = C // 2
+
+        def interleave_v(dst, src):
+            interleave(vcopy, dst[:, :half, :], src[:, :, :half])
+
+        def interleave_s(dst, src):
+            interleave(scopy, dst[:, half:, :], src[:, :, half:])
+
         for j in range(J):
             gather(0, j)
         interleave(scopy, gb[0][:], g4[0][:])
-        group_w2(vcopy, 0, 0, 2)
-        group_w2(scopy, 0, 2, 4)
-        quant_w2(0)
-        quant_g(0)
-        dh = first_product(0)
-        make_da(0, dh)
-        interleave_shared(dab[0][:], da4[0][:])
-        quant_da(0)
-        interleave(scopy, w1b[0][:], w1_raw[0][:])
-        quant_w1(0)
-        second_product(0)
-        for j in range(J):
+        for j in range(J - 1):
             gather(1, j)
+        group_w2(scopy, 0, 0, P)
+        quant_g(0)
+        gather(1, J - 1)
+        interleave(scopy, w1b[0][:], w1_raw[0][:])
+        quant_w2(0)
         interleave(scopy, gb[1][:], g4[1][:])
-        group_w2(scopy, 1, 0, 4)
-        quant_w2(1)
+        quant_w1(0)
+        dh0 = first_product(0)
+        make_da(0, dh0, range(3))
+        group_w2(scopy, 1, 0, P)
         quant_g(1)
-        dh = first_product(1)
-        make_da(1, dh)
-        interleave_shared(dab[1][:], da4[1][:])
+        make_da(0, dh0, range(3, J))
+        interleave_v(dab[0][:], da4[0][:])
+        interleave_s(dab[0][:], da4[0][:])
+        quant_w2(1)
         interleave(scopy, w1b[1][:], w1_raw[1][:])
+        dh1 = first_product(1)
+        quant_da(0)
+        make_da(1, dh1)
+        dx0 = second_product(0)
+        emit_dx(0, 0, dx0)
         quant_w1(1)
+        interleave_v(dab[1][:], da4[1][:])
+        interleave_s(dab[1][:], da4[1][:])
+        emit_dx(0, 1, dx0)
         scatter(0, 0)
         quant_da(1)
         scatter(0, 1)
-        second_product(1)
+        dx1 = second_product(1)
         for m in range(2):
+            emit_dx(1, m, dx1)
             scatter(1, m)
             nc.sync.dma_start(out=out[m * P : (m + 1) * P, :], in_=outs[m][:])

@@ -19,7 +19,7 @@ COPY = mybir.ActivationFunctionType.Copy
 
 P = 128
 J = 4
-DX_BANK = ((0, 7), (1, 2))
+DX_BANK = ((0, 1), (4, 5))
 
 
 def tile_moe_bdx_mlp_relu2_kernel(tc, dyT, a, w2, w1, gate, offs, out):
@@ -62,11 +62,11 @@ def tile_moe_bdx_mlp_relu2_kernel(tc, dyT, a, w2, w1, gate, offs, out):
             nc.sync.dma_start(out=dy[j][:], in_=dyv[j])
         load_gate(1)
         load_w2(0)
-        load_w1(0)
-        load_w1(1)
-        load_a(0)
         load_w2(1)
+        load_a(0)
+        load_w1(0)
         load_a(1)
+        load_w1(1)
 
         g4 = [sb([P, J, C], F32, f"g4_{e}") for e in range(E)]
         gb = [sb([P, C, J], BF16, f"gb{e}") for e in range(E)]
@@ -82,7 +82,8 @@ def tile_moe_bdx_mlp_relu2_kernel(tc, dyT, a, w2, w1, gate, offs, out):
         dab = [sb([P, C, J], BF16, f"dab{e}") for e in range(E)]
         daq = [sb([P, C], U32, f"daq{e}") for e in range(E)]
         das = [sb([P, C], U8, f"das{e}") for e in range(E)]
-        dx = [[sb([P, C], F32, f"dx{e}_{m}") for m in range(2)] for e in range(E)]
+        relu1 = sb([P, 2, C], F32, "relu1")
+        dh_copy = [sb([P, C], F32, f"dh_copy{i}") for i in range(2)]
         outs = [sb([P, T], F32, f"outs{m}") for m in range(2)]
 
         def offs_of(e):
@@ -115,9 +116,9 @@ def tile_moe_bdx_mlp_relu2_kernel(tc, dyT, a, w2, w1, gate, offs, out):
         def quant_da(e):
             quantize(daq[e], das[e], dab[e][:].rearrange("p c j -> p (c j)"), E5M2X4)
 
-        def first_product(e):
-            banks = []
-            for t in range(J):
+        def first_product(e, order=range(J)):
+            banks = {}
+            for t in order:
                 bank = psum.tile([P, C], F32, name=f"dh{e}_{t}", tag=f"bank{4 * e + t}")
                 cols = slice(t * P, (t + 1) * P)
                 nc.tensor.matmul_mx(
@@ -129,7 +130,7 @@ def tile_moe_bdx_mlp_relu2_kernel(tc, dyT, a, w2, w1, gate, offs, out):
                     start=True,
                     stop=True,
                 )
-                banks.append(bank)
+                banks[t] = bank
             return banks
 
         def make_da(e, banks, ts=range(J)):
@@ -155,21 +156,18 @@ def tile_moe_bdx_mlp_relu2_kernel(tc, dyT, a, w2, w1, gate, offs, out):
                 sums.append(bank)
             return sums
 
-        def emit_dx(e, m, sums):
-            nc.scalar.activation(dx[e][m][:], sums[m][:], COPY, scale=2.0)
+        def emit_dx(e, m, sums, lo=0, hi=C, tag=None):
+            tile = keep.tile([P, hi - lo], F32, name=f"dx{e}_{m}_{lo}", tag=tag or f"dx{e}_{m}_{lo}", align_bytes=64)
+            nc.scalar.activation(tile[:], sums[m][:, lo:hi], COPY, scale=2.0)
+            return tile
 
-        def scatter(e, m):
-            nc.vector.tensor_copy(outs[m][:].indirect(offs_of(e)), dx[e][m][:])
+        def scatter(e, m, tile, lo=0, hi=C):
+            first = (e * C + lo) // 16
+            last = (e * C + hi) // 16
+            nc.vector.tensor_copy(outs[m][:].indirect(offsets[:, first:last]), tile[:, : hi - lo])
 
         scopy = nc.scalar.copy
         vcopy = nc.vector.tensor_copy
-
-        half = C // 2
-
-        def interleave_shared(dst, src):
-            interleave(vcopy, dst[:, :half, :], src[:, :, :half])
-            interleave(scopy, dst[:, half:, :], src[:, :, half:])
-
         half = C // 2
 
         def interleave_v(dst, src):
@@ -186,33 +184,36 @@ def tile_moe_bdx_mlp_relu2_kernel(tc, dyT, a, w2, w1, gate, offs, out):
         group_w2(scopy, 0, 0, P)
         quant_g(0)
         gather(1, J - 1)
-        interleave(scopy, w1b[0][:], w1_raw[0][:])
         quant_w2(0)
         interleave(scopy, gb[1][:], g4[1][:])
-        quant_w1(0)
         dh0 = first_product(0)
         make_da(0, dh0, range(3))
+        interleave(nc.gpsimd.tensor_copy, w1b[0][:], w1_raw[0][:])
         group_w2(scopy, 1, 0, P)
         quant_g(1)
         make_da(0, dh0, range(3, J))
+        quant_w2(1)
+        dh1 = first_product(1, (2, 3, 0, 1))
         interleave_v(dab[0][:], da4[0][:])
         interleave_s(dab[0][:], da4[0][:])
-        quant_w2(1)
-        interleave(scopy, w1b[1][:], w1_raw[1][:])
-        dh1 = first_product(1)
+        quant_w1(0)
+        nc.scalar.activation(relu1[:], a_raw[1][:, 2:4, :], mybir.ActivationFunctionType.Relu)
         quant_da(0)
-        make_da(1, dh1)
         dx0 = second_product(0)
-        emit_dx(0, 0, dx0)
+        for i in range(2):
+            nc.scalar.copy(dh_copy[i][:], dh1[2 + i][:])
+            nc.gpsimd.tensor_tensor(out=da4[1][:, 2 + i, :], in0=relu1[:, i, :], in1=dh_copy[i][:], op=MULT)
+        make_da(1, dh1, range(2))
+        d00 = emit_dx(0, 0, dx0)
+        interleave(scopy, w1b[1][:], w1_raw[1][:])
         quant_w1(1)
-        interleave_v(dab[1][:], da4[1][:])
-        interleave_s(dab[1][:], da4[1][:])
-        emit_dx(0, 1, dx0)
-        scatter(0, 0)
+        scatter(0, 0, d00)
+        interleave(scopy, dab[1][:], da4[1][:])
         quant_da(1)
-        scatter(0, 1)
+        d01 = emit_dx(0, 1, dx0, 0, C, tag="da4_1")
+        scatter(0, 1, d01)
         dx1 = second_product(1)
         for m in range(2):
-            emit_dx(1, m, dx1)
-            scatter(1, m)
+            d1 = emit_dx(1, m, dx1)
+            scatter(1, m, d1)
             nc.sync.dma_start(out=out[m * P : (m + 1) * P, :], in_=outs[m][:])

from contextlib import ExitStack

import concourse.mybir as mybir

K, T, E, C, H, N = 256, 1024, 2, 512, 512, 512
FLOPS = 2 * E * C * (N * H + H * K)
BYTES = 4 * (N * T + H * E * C + E * N * H + E * H * K + E * C + K * T) + 2 * T * 8

F32 = mybir.dt.float32
BF16 = mybir.dt.bfloat16
U32 = mybir.dt.uint32
U16 = mybir.dt.uint16
U8 = mybir.dt.uint8
E4M3X4 = mybir.dt.float8_e4m3fn_x4
E5M2X4 = mybir.dt.float8_e5m2_x4
MULT = mybir.AluOpType.mult
MAX = mybir.AluOpType.max
COPY = mybir.ActivationFunctionType.Copy

P = 128
J = 4
DX_BANK = ((0, 1), (4, 5))


def tile_moe_bdx_mlp_relu2_kernel(tc, dyT, a, w2, w1, gate, offs, out):
    nc = tc.nc
    with ExitStack() as ctx:
        keep = ctx.enter_context(tc.tile_pool(name="keep", bufs=1))
        psum = ctx.enter_context(tc.psum_pool(name="psum", bufs=1))

        def sb(shape, dtype, name):
            return keep.tile(shape, dtype, name=name, align_bytes=64)

        offsets = keep.tile([P, T // 16], U16, name="offsets")
        gates = [sb([P, C], F32, f"gate{e}") for e in range(E)]
        dy = [sb([P, T], F32, f"dy{j}") for j in range(J)]
        w2_raw = [sb([P, J, H], F32, f"w2_raw{e}") for e in range(E)]
        w1_raw = [sb([P, J, K], F32, f"w1_raw{e}") for e in range(E)]
        a_raw = [sb([P, J, C], F32, f"a_raw{e}") for e in range(E)]

        dyv = dyT.rearrange("(p j) t -> j p t", j=J)
        av = a.rearrange("(p j) s -> p j s", j=J)

        def slots(e):
            return slice(e * C, (e + 1) * C)

        def load_gate(e):
            nc.sync.dma_start(out=gates[e][:], in_=gate[0:P, slots(e)])

        def load_w2(e):
            nc.sync.dma_start(out=w2_raw[e][:], in_=w2[e].rearrange("(p j) i -> p j i", j=J))

        def load_w1(e):
            nc.sync.dma_start(out=w1_raw[e][:], in_=w1[e].rearrange("(p j) k -> p j k", j=J))

        def load_a(e):
            nc.sync.dma_start(out=a_raw[e][:], in_=av[:, :, slots(e)])

        nc.sync.dma_start(offsets[:], offs)
        load_gate(0)
        for j in range(J):
            nc.sync.dma_start(out=dy[j][:], in_=dyv[j])
        load_gate(1)
        load_w2(0)
        load_w2(1)
        load_a(0)
        load_w1(0)
        load_a(1)
        load_w1(1)

        g4 = [sb([P, J, C], F32, f"g4_{e}") for e in range(E)]
        gb = [sb([P, C, J], BF16, f"gb{e}") for e in range(E)]
        gq = [sb([P, C], U32, f"gq{e}") for e in range(E)]
        gs = [sb([P, C], U8, f"gs{e}") for e in range(E)]
        w2b = [sb([P, J, P, J], BF16, f"w2b{e}") for e in range(E)]
        w2q = [sb([P, H], U32, f"w2q{e}") for e in range(E)]
        w2s = [sb([P, H], U8, f"w2s{e}") for e in range(E)]
        w1b = [sb([P, K, J], BF16, f"w1b{e}") for e in range(E)]
        w1q = [sb([P, K], U32, f"w1q{e}") for e in range(E)]
        w1s = [sb([P, K], U8, f"w1s{e}") for e in range(E)]
        da4 = [sb([P, J, C], BF16, f"da4_{e}") for e in range(E)]
        dab = [sb([P, C, J], BF16, f"dab{e}") for e in range(E)]
        daq = [sb([P, C], U32, f"daq{e}") for e in range(E)]
        das = [sb([P, C], U8, f"das{e}") for e in range(E)]
        relu1 = sb([P, 2, C], F32, "relu1")
        dh_copy = [sb([P, C], F32, f"dh_copy{i}") for i in range(2)]
        outs = [sb([P, T], F32, f"outs{m}") for m in range(2)]

        def offs_of(e):
            return offsets[:, e * (C // 16) : (e + 1) * (C // 16)]

        def gather(e, j):
            nc.vector.tensor_tensor(g4[e][:, j, :], dy[j][:].indirect(offs_of(e)), gates[e][:], MULT)

        def interleave(copy, dst, src):
            copy(out=dst.rearrange("p (c i) t -> p c t i", i=4), in_=src.rearrange("p t (c i) -> p c t i", i=4))

        def group_w2(copy, e, m0, m1):
            copy(
                out=w2b[e][:].rearrange("p t m j -> p m j t")[:, m0:m1],
                in_=w2_raw[e][:].rearrange("p j (m t) -> p m j t", t=4)[:, m0:m1],
            )

        def quantize(codes, scales, src, fmt):
            nc.vector.quantize_mx(out=codes[:].bitcast(fmt), scales=scales[:], in_=src)

        def quant_w2(e):
            quantize(w2q[e], w2s[e], w2b[e][:].rearrange("p t m j -> p (t m j)"), E4M3X4)

        def quant_w1(e):
            quantize(w1q[e], w1s[e], w1b[e][:].rearrange("p k j -> p (k j)"), E4M3X4)

        def quant_g(e):
            quantize(gq[e], gs[e], gb[e][:].rearrange("p c j -> p (c j)"), E5M2X4)

        def quant_da(e):
            quantize(daq[e], das[e], dab[e][:].rearrange("p c j -> p (c j)"), E5M2X4)

        def first_product(e, order=range(J)):
            banks = {}
            for t in order:
                bank = psum.tile([P, C], F32, name=f"dh{e}_{t}", tag=f"bank{4 * e + t}")
                cols = slice(t * P, (t + 1) * P)
                nc.tensor.matmul_mx(
                    out=bank[:],
                    lhsT=w2q[e][:, cols].bitcast(E4M3X4),
                    lhsT_scale=w2s[e][:, cols],
                    rhs=gq[e][:].bitcast(E5M2X4),
                    rhs_scale=gs[e][:],
                    start=True,
                    stop=True,
                )
                banks[t] = bank
            return banks

        def make_da(e, banks, ts=range(J)):
            for t in ts:
                nc.vector.scalar_tensor_tensor(
                    out=da4[e][:, t, :], in0=a_raw[e][:, t, :], scalar=0.0, in1=banks[t][:], op0=MAX, op1=MULT
                )

        def second_product(e):
            sums = []
            for m in range(2):
                bank = psum.tile([P, C], F32, name=f"dxp{e}_{m}", tag=f"bank{DX_BANK[e][m]}")
                cols = slice(m * P, (m + 1) * P)
                nc.tensor.matmul_mx(
                    out=bank[:],
                    lhsT=w1q[e][:, cols].bitcast(E4M3X4),
                    lhsT_scale=w1s[e][:, cols],
                    rhs=daq[e][:].bitcast(E5M2X4),
                    rhs_scale=das[e][:],
                    start=True,
                    stop=True,
                )
                sums.append(bank)
            return sums

        def emit_dx(e, m, sums, lo=0, hi=C, tag=None):
            tile = keep.tile([P, hi - lo], F32, name=f"dx{e}_{m}_{lo}", tag=tag or f"dx{e}_{m}_{lo}", align_bytes=64)
            nc.scalar.activation(tile[:], sums[m][:, lo:hi], COPY, scale=2.0)
            return tile

        def scatter(e, m, tile, lo=0, hi=C):
            first = (e * C + lo) // 16
            last = (e * C + hi) // 16
            nc.vector.tensor_copy(outs[m][:].indirect(offsets[:, first:last]), tile[:, : hi - lo])

        scopy = nc.scalar.copy
        vcopy = nc.vector.tensor_copy
        half = C // 2

        def interleave_v(dst, src):
            interleave(vcopy, dst[:, :half, :], src[:, :, :half])

        def interleave_s(dst, src):
            interleave(scopy, dst[:, half:, :], src[:, :, half:])

        for j in range(J):
            gather(0, j)
        interleave(scopy, gb[0][:], g4[0][:])
        for j in range(J - 1):
            gather(1, j)
        group_w2(scopy, 0, 0, P)
        quant_g(0)
        gather(1, J - 1)
        quant_w2(0)
        interleave(scopy, gb[1][:], g4[1][:])
        dh0 = first_product(0)
        make_da(0, dh0, range(3))
        interleave(nc.gpsimd.tensor_copy, w1b[0][:], w1_raw[0][:])
        group_w2(scopy, 1, 0, P)
        quant_g(1)
        make_da(0, dh0, range(3, J))
        quant_w2(1)
        dh1 = first_product(1, (2, 3, 0, 1))
        interleave_v(dab[0][:], da4[0][:])
        interleave_s(dab[0][:], da4[0][:])
        quant_w1(0)
        nc.scalar.activation(relu1[:], a_raw[1][:, 2:4, :], mybir.ActivationFunctionType.Relu)
        quant_da(0)
        dx0 = second_product(0)
        for i in range(2):
            nc.scalar.copy(dh_copy[i][:], dh1[2 + i][:])
            nc.gpsimd.tensor_tensor(out=da4[1][:, 2 + i, :], in0=relu1[:, i, :], in1=dh_copy[i][:], op=MULT)
        make_da(1, dh1, range(2))
        d00 = emit_dx(0, 0, dx0)
        interleave(scopy, w1b[1][:], w1_raw[1][:])
        quant_w1(1)
        scatter(0, 0, d00)
        interleave(scopy, dab[1][:], da4[1][:])
        quant_da(1)
        d01 = emit_dx(0, 1, dx0, 0, C, tag="da4_1")
        scatter(0, 1, d01)
        dx1 = second_product(1)
        for m in range(2):
            d1 = emit_dx(1, m, dx1)
            scatter(1, m, d1)
            nc.sync.dma_start(out=out[m * P : (m + 1) * P, :], in_=outs[m][:])
